import numpy as np
import ml_dtypes


def mxq(x, axis, fmt="e4m3"):
    dtype, down = {"e4m3": (ml_dtypes.float8_e4m3fn, 7), "e5m2": (ml_dtypes.float8_e5m2, 14)}[fmt]
    v = np.moveaxis(np.asarray(x, np.float32).astype(ml_dtypes.bfloat16).astype(np.float64), axis, -1)
    blocks = v.reshape(v.shape[:-1] + (-1, 32))
    amax = np.abs(blocks).max(-1, keepdims=True)
    byte = np.maximum(np.where(amax > 0, np.frexp(amax)[1] - 1 + 127, 0) - down, 1)
    scale = np.exp2(byte - 127.0)
    codes = (blocks / scale).astype(np.float32).astype(dtype).astype(np.float64)
    return np.moveaxis((codes * scale).reshape(v.shape), -1, axis)


WIDE = False


def mx_kscale(k):
    if not WIDE:
        return np.ones(k)
    levels = np.array([30, -30])
    if k % 512:
        return np.exp2(np.random.permutation(np.resize(levels, k // 32))).repeat(32)
    a = np.empty((k // 512, 16))
    for p in range(k // 512):
        a[p, :8] = np.random.permutation(np.resize(levels, 8))
        for g in range(8):
            far = levels[np.abs(levels - a[p, g]) >= 10]
            a[p, g + 8] = far[np.random.randint(len(far))]
    return np.exp2(a.ravel()).repeat(32)


def f64(x):
    return np.asarray(x).astype(np.float64)


def striped(idx):
    return np.tile(np.asarray(idx).reshape(-1, 16).T, (8, 1)).astype(np.uint16)


def unstriped(offs):
    return offs[:16].T.reshape(-1).astype(np.int64)


E2M1 = np.array([0.0, 0.5, 1.0, 1.5, 2.0, 3.0, 4.0, 6.0, -0.0, -0.5, -1.0, -1.5, -2.0, -3.0, -4.0, -6.0])


def pack_weight(w, fmt):
    k, n = w.shape
    w = f64(np.asarray(w, np.float32).astype(ml_dtypes.bfloat16)).reshape(k // 32, 32, n)
    amax = np.abs(w).max(1)
    if fmt in ("e4m3", "e5m2"):
        byte = np.frexp(amax)[1] - 1 + 127 - (7 if fmt == "e4m3" else 14)
    else:
        mant, ex = np.frexp(amax / 6.0)
        byte = np.where(mant > 0.5, ex, ex - 1) + 127
    byte = np.clip(np.where(amax > 0, byte, 1), 1, 254)
    scaled = (w * np.exp2(127.0 - byte)[:, None, :]).reshape(k, n).astype(np.float32)
    by_word = np.ascontiguousarray(scaled.reshape(k // 512, 128, 4, n).transpose(0, 1, 3, 2))
    if fmt in ("e4m3", "e5m2"):
        words = by_word.astype(ml_dtypes.float8_e4m3fn if fmt == "e4m3" else ml_dtypes.float8_e5m2).view(np.uint8)
    else:
        c = by_word.astype(ml_dtypes.float4_e2m1fn).view(np.uint8) & 0xF
        words = (c[..., 0::2] | (c[..., 1::2] << 4)).reshape(k // 512, 128, 2 * n)
    return np.ascontiguousarray(words), np.ascontiguousarray(byte.astype(np.uint8).reshape(k // 512, 16, n))


def unpack_weight(words, scales, fmt):
    g, _, n = scales.shape
    words = np.ascontiguousarray(words).reshape(g, 128, n, -1)
    if fmt in ("e4m3", "e5m2"):
        vals = words.view(ml_dtypes.float8_e4m3fn if fmt == "e4m3" else ml_dtypes.float8_e5m2).astype(np.float64)
    else:
        nib = np.empty((g, 128, n, 4), np.uint8)
        nib[..., 0::2] = words & 0xF
        nib[..., 1::2] = words >> 4
        vals = E2M1[nib]
    vals = vals * np.repeat(np.exp2(scales.astype(np.float64) - 127.0), 8, axis=1)[..., None]
    return vals.transpose(0, 1, 3, 2).reshape(g * 512, n)


K, T, J, R, F, Z, O, N, E = 512, 1024, 256, 512, 512, 1024, 128, 256, 1024


def setup_inputs():
    n = np.random.standard_normal
    idx = np.random.permutation(T)[:J]
    idx2 = np.random.permutation(Z)[:J]
    idx3 = np.random.permutation(J)[:O]
    idx4 = np.random.permutation(J)[:O]
    idx5 = np.random.permutation(J)[:O]
    idx6 = np.random.permutation(T)[:O]
    idx7 = np.random.permutation(E)[:O]
    fk = mx_kscale(K)
    ff = mx_kscale(F)
    fr = mx_kscale(R)
    xtp = pack_weight(n((K, T)) / fk[:, None], "e4m3")
    xop = pack_weight(n((F, Z)) / ff[:, None], "e2m1")
    wp = pack_weight(n((K, R)) * 1 / np.sqrt(K) * fk[:, None] * fr, "e2m1")
    w2p = pack_weight(n((K, R)) * 1 / np.sqrt(K) * fk[:, None], "e5m2")
    w0p = pack_weight(n((F, R)) * 1 / np.sqrt(F) * ff[:, None], "e5m2")
    wbp = pack_weight(n((R, N)) * 1 / np.sqrt(R) / fr[:, None], "e5m2")
    wsp = pack_weight(n((K, N)) * 1 / np.sqrt(K) * fk[:, None], "e5m2")
    return {
        "xt_words": xtp[0],
        "xt_scales": xtp[1],
        "xo_words": xop[0],
        "xo_scales": xop[1],
        "w_words": wp[0],
        "w_scales": wp[1],
        "w2_words": w2p[0],
        "w2_scales": w2p[1],
        "w0_words": w0p[0],
        "w0_scales": w0p[1],
        "wb_words": wbp[0],
        "wb_scales": wbp[1],
        "ws_words": wsp[0],
        "ws_scales": wsp[1],
        "offs": striped(idx),
        "offs2": striped(idx2),
        "offs3": striped(idx3),
        "offs4": striped(idx4),
        "offs5": striped(idx5),
        "offs6": striped(idx6),
        "offs7": striped(idx7),
    }


def reference(xt_words, xt_scales, xo_words, xo_scales, w_words, w_scales, w2_words, w2_scales, w0_words, w0_scales, wb_words, wb_scales, ws_words, ws_scales, offs, offs2, offs3, offs4, offs5, offs6, offs7):
    idx = unstriped(offs)
    idx2 = unstriped(offs2)
    idx3 = unstriped(offs3)
    idx4 = unstriped(offs4)
    idx5 = unstriped(offs5)
    idx6 = unstriped(offs6)
    idx7 = unstriped(offs7)
    xtu = unpack_weight(xt_words, xt_scales, "e4m3")
    xou = unpack_weight(xo_words, xo_scales, "e2m1")
    wu = unpack_weight(w_words, w_scales, "e2m1")
    w2u = unpack_weight(w2_words, w2_scales, "e5m2")
    w0u = unpack_weight(w0_words, w0_scales, "e5m2")
    wbu = unpack_weight(wb_words, wb_scales, "e5m2")
    wsu = unpack_weight(ws_words, ws_scales, "e5m2")
    xtidxg = xtu[:, idx]
    a = wu.T @ xtidxg
    xoidx2g = xou[:, idx2]
    b = w2u.T @ xtidxg + w0u.T @ xoidx2g
    lb = b[:, 0:1]
    lb2 = b[:, 128:129]
    la = a[:, 0:1]
    hid = np.maximum(a[:, idx3] * lb, a[:, idx4] * lb2) - b[:, idx5] * la
    hidq = mxq(hid, 0, "e4m3")
    xtidx6g = xtu[:, idx6]
    p = wbu.T @ hidq + wsu.T @ xtidx6g
    y = np.zeros((N, E))
    y[:, idx7] = p
    return y

from contextlib import ExitStack

import concourse.mybir as mybir

K, T, J, R, F, Z, O, N, E = 512, 1024, 256, 512, 512, 1024, 128, 256, 1024
FLOPS = 2 * (K * R * J + K * R * J + F * R * J + R * N * O + K * N * O)

F32 = mybir.dt.float32
BF16 = mybir.dt.bfloat16
I32 = mybir.dt.int32
U32 = mybir.dt.uint32
U16 = mybir.dt.uint16
U8 = mybir.dt.uint8
E4M3 = mybir.dt.float8_e4m3fn_x4
E5M2 = mybir.dt.float8_e5m2_x4
E2M1 = mybir.dt.float4_e2m1fn_x4
COPY = mybir.ActivationFunctionType.Copy
MAX = mybir.AluOpType.max
SUBTRACT = mybir.AluOpType.subtract

P = 128
PACK = 4
QUADS = 4
QUAD = 32
ALIGN = 64


def tile_list_leadthree_leaned_further_scattered_kernel(
    tc, xt_words, xt_scales, xo_words, xo_scales, w_words, w_scales, w2_words, w2_scales, w0_words, w0_scales,
    wb_words, wb_scales, ws_words, ws_scales, offs, offs2, offs3, offs4, offs5, offs6, offs7, out,
):
    nc = tc.nc
    with ExitStack() as ctx:
        sb = ctx.enter_context(tc.tile_pool(name="sb", bufs=1))
        ps = ctx.enter_context(tc.psum_pool(name="ps", bufs=1))

        def sbuf(name, shape, dtype, tag=None):
            return sb.tile(shape, dtype, name=name, tag=tag or name, align_bytes=ALIGN)

        def load_list(name, src):
            tile = sb.tile(list(src.shape), U16, name=name)
            nc.sync.dma_start(tile[:], src)
            return tile

        def load_fp8_words(queue, tile, src):
            queue.dma_start(tile[:], src[0].rearrange("p n t -> p (n t)").bitcast(I32))

        def load_fp4_words(queue, tile, src):
            queue.dma_start(tile[:].bitcast(I32), src[0].bitcast(I32))

        def load_scale_quadrant(queue, plane, src, q):
            queue.dma_start(
                plane[QUAD * q : QUAD * q + PACK, :].bitcast(I32),
                src[0, PACK * q : PACK * (q + 1), :].bitcast(I32),
            )

        def load_staged_scales(queue, slot, src):
            words = R // 4
            queue.dma_start(
                staged[:, :, slot * words : (slot + 1) * words],
                src[0].bitcast(I32).rearrange("(q r) n -> r q n", r=PACK),
            )

        xt_w = sbuf("xt_w", [P, T], I32)
        xt_s = sbuf("xt_s", [P, T], U8)
        xo_w = sbuf("xo_w", [P, Z], U16)
        xo_s = sbuf("xo_s", [P, Z], U8)
        w_w = sbuf("w_w", [P, R], U16)
        w2_w = sbuf("w2_w", [P, R], I32)
        w0_w = sbuf("w0_w", [P, R], I32)
        wb_w = sbuf("wb_w", [P, N], I32)
        wb_s = sbuf("wb_s", [P, N], U8)
        ws_w = sbuf("ws_w", [P, N], I32)
        ws_s = sbuf("ws_s", [P, N], U8)
        staged = sbuf("staged", [PACK, QUADS, 3 * R // 4], I32)
        first_s = sbuf("first_s", [P, 3 * R], U8)
        pages = [sbuf(f"page{h}", [P, E], F32) for h in range(2)]

        nc.vector.memset(xt_s[:].bitcast(I32), 0)
        nc.vector.memset(xo_s[:].bitcast(I32), 0)
        nc.vector.memset(first_s[:].bitcast(I32), 0)
        nc.vector.memset(ws_s[:].bitcast(I32), 0)
        nc.vector.memset(wb_s[:].bitcast(I32), 0)
        for page in pages:
            nc.vector.memset(page[:], 0.0)

        load_staged_scales(nc.sync, 0, w_scales)
        load_staged_scales(nc.scalar, 1, w2_scales)
        l1 = load_list("l1", offs)
        load_staged_scales(nc.scalar, 2, w0_scales)
        load_fp8_words(nc.sync, xt_w, xt_words)
        load_fp4_words(nc.scalar, w_w, w_words)
        load_fp8_words(nc.sync, w2_w, w2_words)
        load_fp4_words(nc.scalar, xo_w, xo_words)
        for q in range(QUADS):
            load_scale_quadrant(nc.sync, xt_s, xt_scales, q)
        l2 = load_list("l2", offs2)
        load_fp8_words(nc.sync, w0_w, w0_words)
        for q in range(QUADS):
            load_scale_quadrant(nc.sync, xo_s, xo_scales, q)
        l3 = load_list("l3", offs3)
        l4 = load_list("l4", offs4)
        l5 = load_list("l5", offs5)
        l6 = load_list("l6", offs6)
        load_fp8_words(nc.sync, ws_w, ws_words)
        for q in range(QUADS):
            load_scale_quadrant(nc.sync, ws_s, ws_scales, q)
        load_fp8_words(nc.sync, wb_w, wb_words)
        for q in range(QUADS):
            load_scale_quadrant(nc.sync, wb_s, wb_scales, q)
        l7 = load_list("l7", offs7)

        for q in range(QUADS):
            nc.vector.tensor_copy(first_s[QUAD * q : QUAD * q + PACK, :].bitcast(I32), staged[:, q, :])
        dealt_first = sbuf("dealt_first", [P, 3 * P], U8)
        dealt_s = [dealt_first[:]]

        def deal_scales(t):
            nc.vector.tensor_copy(dealt_s[t], first_s[:, t::PACK])

        def deal_words(name, words, dtype, run):
            halves = []
            src = words.rearrange("p (c i t) -> p c t i", i=run, t=PACK)
            for u in range(2):
                half = sbuf(f"{name}{u}", [P, 2 * P], dtype)
                nc.scalar.copy(half[:].rearrange("p (t c i) -> p c t i", t=2, i=run), src[:, :, 2 * u : 2 * u + 2, :])
                halves.append(half)
            return [halves[t // 2][:, (t % 2) * P : (t % 2 + 1) * P] for t in range(PACK)]

        def gather(name, window, offsets, count, dtype):
            tile = sbuf(name, [P, count], dtype)
            nc.vector.tensor_copy(tile[:], window.indirect(offsets[:]))
            return tile

        deal_scales(0)
        w_t = deal_words("w_t", w_w[:], U16, 8)
        xg_w = gather("xg_w", xt_w[:].bitcast(U32), l1, J, U32)
        xg_s = gather("xg_s", xt_s[:], l1, J, U8)
        w2_t = deal_words("w2_t", w2_w[:].bitcast(U32), U32, 4)
        w0_t = deal_words("w0_t", w0_w[:].bitcast(U32), U32, 4)
        og_w = gather("og_w", xo_w[:], l2, J, U16)
        og_s = gather("og_s", xo_s[:], l2, J, U8)
        dealt_rest = sbuf("dealt_rest", [P, 3 * 3 * P], U8, tag="xo_s")
        dealt_s.extend(dealt_rest[:, 3 * P * u : 3 * P * (u + 1)] for u in range(PACK - 1))
        deal_scales(1)
        deal_scales(2)
        deal_scales(3)

        a_ps = [ps.tile([P, J], F32, name=f"a_ps{t}", tag=f"bank{t}") for t in range(PACK)]
        b_ps = [ps.tile([P, J], F32, name=f"b_ps{t}", tag=f"bank{PACK + t}") for t in range(PACK)]
        a_sb = [sbuf(f"a_sb{t}", [P, J], F32) for t in range(PACK)]
        b_sb = [sbuf(f"b_sb{t}", [P, J], F32) for t in range(PACK)]
        for t in range(PACK):
            nc.tensor.matmul_mx(
                out=a_ps[t][:], lhsT=w_t[t].bitcast(E2M1), lhsT_scale=dealt_s[t][:, 0:P],
                rhs=xg_w[:].bitcast(E4M3), rhs_scale=xg_s[:], start=True, stop=True,
            )
            nc.tensor.matmul_mx(
                out=b_ps[t][:], lhsT=w2_t[t].bitcast(E5M2), lhsT_scale=dealt_s[t][:, P : 2 * P],
                rhs=xg_w[:].bitcast(E4M3), rhs_scale=xg_s[:], start=True, stop=False,
            )
            nc.tensor.matmul_mx(
                out=b_ps[t][:], lhsT=w0_t[t].bitcast(E5M2), lhsT_scale=dealt_s[t][:, 2 * P : 3 * P],
                rhs=og_w[:].bitcast(E2M1), rhs_scale=og_s[:], start=False, stop=True,
            )

        hid = sbuf("hid", [P, O, PACK], BF16)
        look3 = [sbuf(f"look3_{u}", [P, 2, O], F32) for u in range(2)]
        look4 = [sbuf(f"look4_{u}", [P, 2, O], F32) for u in range(2)]
        look5 = [sbuf(f"look5_{u}", [P, 2, O], F32) for u in range(2)]
        larger = [sbuf(f"larger{u}", [P, 2, O], F32) for u in range(2)]

        def looks(t):
            u, s = divmod(t, 2)
            nc.scalar.activation(out=look3[u][:, s, :], in_=a_sb[t][:].indirect(l3[:]), func=COPY, scale=b_sb[t][:, 0:1])
            nc.scalar.activation(out=look4[u][:, s, :], in_=a_sb[t][:].indirect(l4[:]), func=COPY, scale=b_sb[t][:, 128:129])
            nc.scalar.activation(out=look5[u][:, s, :], in_=b_sb[t][:].indirect(l5[:]), func=COPY, scale=a_sb[t][:, 0:1])

        def combine(u):
            nc.vector.tensor_tensor(larger[u][:], look3[u][:], look4[u][:], MAX)
            nc.vector.tensor_tensor(
                hid[:, :, 2 * u : 2 * u + 2],
                larger[u][:].rearrange("p s o -> p o s"),
                look5[u][:].rearrange("p s o -> p o s"),
                SUBTRACT,
            )

        nc.scalar.copy(a_sb[0][:], a_ps[0][:])
        nc.vector.tensor_copy(b_sb[0][:], b_ps[0][:])
        for t in range(1, PACK):
            nc.vector.tensor_copy(a_sb[t][:], a_ps[t][:])
            nc.vector.tensor_copy(b_sb[t][:], b_ps[t][:])
        for t in range(PACK):
            looks(t)
        combine(0)
        x6_w = gather("x6_w", xt_w[:].bitcast(U32), l6, O, U32)
        x6_s = gather("x6_s", xt_s[:], l6, O, U8)
        p_ps = [ps.tile([P, O], F32, name=f"p_ps{h}", tag=f"bank{h}") for h in range(2)]
        for h in range(2):
            cols = slice(h * P, (h + 1) * P)
            nc.tensor.matmul_mx(
                out=p_ps[h][:], lhsT=ws_w[:, cols].bitcast(E5M2), lhsT_scale=ws_s[:, cols],
                rhs=x6_w[:].bitcast(E4M3), rhs_scale=x6_s[:], start=True, stop=False,
            )
        combine(1)

        hid_w = sbuf("hid_w", [P, O], U32)
        hid_s = sbuf("hid_s", [P, O], U8)
        nc.vector.quantize_mx(out=hid_w[:].bitcast(E4M3), scales=hid_s[:], in_=hid[:].rearrange("p o t -> p (o t)"))

        p_sb = [sbuf(f"p_sb{h}", [P, O], F32) for h in range(2)]
        for h in range(2):
            cols = slice(h * P, (h + 1) * P)
            nc.tensor.matmul_mx(
                out=p_ps[h][:], lhsT=wb_w[:, cols].bitcast(E5M2), lhsT_scale=wb_s[:, cols],
                rhs=hid_w[:].bitcast(E4M3), rhs_scale=hid_s[:], start=False, stop=True,
            )
        nc.vector.tensor_copy(p_sb[0][:], p_ps[0][:])
        nc.vector.tensor_copy(pages[0][:].indirect(l7[:]), p_sb[0][:])
        nc.sync.dma_start(out[0:P, :], pages[0][:])
        nc.scalar.copy(p_sb[1][:], p_ps[1][:])
        nc.scalar.activation(out=pages[1][:].indirect(l7[:]), in_=p_sb[1][:], func=COPY)
        nc.scalar.dma_start(out[P : 2 * P, :], pages[1][:])
